import numpy as np
import ml_dtypes


def mxq(x, axis, fmt="e4m3"):
    dtype, down = {"e4m3": (ml_dtypes.float8_e4m3fn, 7), "e5m2": (ml_dtypes.float8_e5m2, 14)}[fmt]
    v = np.moveaxis(np.asarray(x, np.float32).astype(ml_dtypes.bfloat16).astype(np.float64), axis, -1)
    blocks = v.reshape(v.shape[:-1] + (-1, 32))
    amax = np.abs(blocks).max(-1, keepdims=True)
    byte = np.maximum(np.where(amax > 0, np.frexp(amax)[1] - 1 + 127, 0) - down, 1)
    scale = np.exp2(byte - 127.0)
    codes = (blocks / scale).astype(np.float32).astype(dtype).astype(np.float64)
    return np.moveaxis((codes * scale).reshape(v.shape), -1, axis)


WIDE = False


def mx_kscale(k):
    if not WIDE:
        return np.ones(k)
    levels = np.array([10, -10, 5, -5, 0])
    if k % 512:
        return np.exp2(np.random.permutation(np.resize(levels, k // 32))).repeat(32)
    a = np.empty((k // 512, 16))
    for p in range(k // 512):
        a[p, :8] = np.random.permutation(np.resize(levels, 8))
        for g in range(8):
            far = levels[np.abs(levels - a[p, g]) >= 10]
            a[p, g + 8] = far[np.random.randint(len(far))]
    return np.exp2(a.ravel()).repeat(32)


def f64(x):
    return np.asarray(x).astype(np.float64)


def striped(idx):
    return np.tile(idx.reshape(-1, 16).T, (8, 1)).astype(np.uint16)


def unstriped(offs):
    return offs[:16].T.reshape(-1).astype(np.int64)


def pack_weight(w):
    k, n = w.shape
    w = f64(np.asarray(w, np.float32).astype(ml_dtypes.bfloat16)).reshape(k // 32, 32, n)
    amax = np.abs(w).max(1)
    byte = np.clip(np.where(amax > 0, np.frexp(amax)[1] - 1 + 127 - 7, 1), 1, 254)
    scaled = (w * np.exp2(127.0 - byte)[:, None, :]).reshape(k, n).astype(np.float32)
    words = np.ascontiguousarray(scaled.reshape(k // 512, 128, 4, n).transpose(0, 1, 3, 2)).astype(ml_dtypes.float8_e4m3fn).view(np.uint8)
    return words, np.ascontiguousarray(byte.astype(np.uint8).reshape(k // 512, 16, n))


def unpack_weight(words, scales):
    g, p, n, _ = words.shape
    vals = np.ascontiguousarray(words).view(ml_dtypes.float8_e4m3fn).astype(np.float64) * np.repeat(np.exp2(scales.astype(np.float64) - 127.0), 8, axis=1)[..., None]
    return vals.transpose(0, 1, 3, 2).reshape(g * 512, n)


E2M1 = np.array([0.0, 0.5, 1.0, 1.5, 2.0, 3.0, 4.0, 6.0, -0.0, -0.5, -1.0, -1.5, -2.0, -3.0, -4.0, -6.0])


def pack_fp4(w):
    k, n = w.shape
    w = f64(np.asarray(w, np.float32).astype(ml_dtypes.bfloat16)).reshape(k // 32, 32, n)
    amax = np.abs(w).max(1)
    mant, ex = np.frexp(amax / 6.0)
    byte = np.clip(np.where(amax > 0, np.where(mant > 0.5, ex, ex - 1) + 127, 1), 1, 254)
    scaled = (w * np.exp2(127.0 - byte)[:, None, :]).reshape(k, n).astype(np.float32)
    c = np.ascontiguousarray(scaled.reshape(k // 512, 128, 4, n).transpose(0, 1, 3, 2)).astype(ml_dtypes.float4_e2m1fn).view(np.uint8) & 0xF
    words = (c[..., 0::2] | (c[..., 1::2] << 4)).reshape(k // 512, 128, 2 * n)
    return np.ascontiguousarray(words), np.ascontiguousarray(byte.astype(np.uint8).reshape(k // 512, 16, n))


def unpack_fp4(words, scales):
    g, _, n = scales.shape
    words = np.ascontiguousarray(words).reshape(g, 128, n, 2)
    nib = np.empty((g, 128, n, 4), np.uint8)
    nib[..., 0::2] = words & 0xF
    nib[..., 1::2] = words >> 4
    vals = E2M1[nib] * np.repeat(np.exp2(scales.astype(np.float64) - 127.0), 8, axis=1)[..., None]
    return vals.transpose(0, 1, 3, 2).reshape(g * 512, n)


def relu(v):
    return np.maximum(v, 0.0)


K, T, S, N, H = 512, 1024, 512, 128, 512


def setup_inputs():
    n = np.random.standard_normal
    s = mx_kscale(K)[:, None]
    u = mx_kscale(H)
    packed_xT = pack_weight(n((K, T)) * s)
    packed_w1 = pack_fp4(n((K, H)) / np.sqrt(K) / s)
    packed_w2 = pack_fp4(n((K, H)) / np.sqrt(K) / s)
    packed_w3 = pack_fp4(n((H, N)) / np.sqrt(H) / u[:, None])
    return {
        "x_words": packed_xT[0],
        "x_scales": packed_xT[1],
        "w1_words": packed_w1[0],
        "w1_scales": packed_w1[1],
        "w2_words": packed_w2[0],
        "w2_scales": packed_w2[1],
        "minv": (np.random.uniform(0.3, 0.9, (H, S))).astype(np.float32),
        "lam0": (np.random.uniform(0.0, 1.0, (H, S))).astype(np.float32),
        "unit": (np.random.uniform(0.6, 1.4, (H, 1)) * u[:, None]).astype(np.float32),
        "w3_words": packed_w3[0],
        "w3_scales": packed_w3[1],
        "offs": striped(np.random.permutation(T)[:S]),
        "bod": striped(np.random.permutation(S)),
    }


def reference(x_words, x_scales, w1_words, w1_scales, w2_words, w2_scales, minv, lam0, unit, w3_words, w3_scales, offs, bod):
    xq = unpack_weight(x_words, x_scales)[:, unstriped(offs)]
    vt = unpack_fp4(w2_words, w2_scales).T @ xq
    vn = unpack_fp4(w1_words, w1_scales).T @ xq
    lam1 = relu(f64(lam0) - (f64(minv) * vn))
    lo = lam1[:, unstriped(bod)]
    dv = lo * (0.6 * f64(minv))
    lam2 = relu(lam1 - (f64(minv) * (vn + dv)))
    cone = 0.6 * lam2
    fric = np.maximum(np.minimum(-1.0 * (f64(minv) * vt), cone), -1.0 * cone)
    l2b = lam2[:, unstriped(bod)]
    hid = f64(unit) * (fric * l2b - (0.4 * vt))
    return unpack_fp4(w3_words, w3_scales).T @ mxq(hid, 0, "e4m3")

@@ -1,0 +1,213 @@
+from contextlib import ExitStack
+
+import concourse.mybir as mybir
+
+K, T, S, N, H = 512, 1024, 512, 128, 512
+FLOPS = 2 * K * H * S * 2 + 2 * H * N * S
+
+F32 = mybir.dt.float32
+BF16 = mybir.dt.bfloat16
+I32 = mybir.dt.int32
+U32 = mybir.dt.uint32
+U16 = mybir.dt.uint16
+U8 = mybir.dt.uint8
+FP8X4 = mybir.dt.float8_e4m3fn_x4
+FP4X4 = mybir.dt.float4_e2m1fn_x4
+ALU = mybir.AluOpType
+ACT = mybir.ActivationFunctionType
+
+P = 128
+PACK = 4
+MU = 0.6
+DRAG = 0.4
+HALF = S // 2
+OUT_CHUNKS = ((0, 256), (256, 384), (384, 512))
+
+
+def load_scale_rows(queue, plane, rows):
+    for q in range(4):
+        queue.dma_start(out=plane[32 * q : 32 * q + 4, :].bitcast(I32), in_=rows[4 * q : 4 * q + 4, :].bitcast(I32))
+
+
+def tile_picked_ycontc_slide_p_kernel(
+    tc, x_words, x_scales, w1_words, w1_scales, w2_words, w2_scales, minv, lam0, unit, w3_words, w3_scales, offs, bod, out
+):
+    nc = tc.nc
+    with ExitStack() as ctx:
+        keep = ctx.enter_context(tc.tile_pool(name="keep", bufs=1))
+        psum = ctx.enter_context(tc.psum_pool(name="psum", bufs=1))
+
+        def plane_tiles(name, dtype=F32):
+            return [keep.tile([P, S], dtype, name="%s%d" % (name, t), align_bytes=64) for t in range(PACK)]
+
+        offs_sb = keep.tile([P, S // 16], U16, name="offs_sb")
+        bod_sb = keep.tile([P, S // 16], U16, name="bod_sb")
+        xw = keep.tile([P, T], I32, name="xw", align_bytes=64)
+        xs = keep.tile([P, T], U8, name="xs", align_bytes=64)
+        w_raw = [keep.tile([P, 2 * H], U8, name="w_raw%d" % i, align_bytes=64) for i in range(2)]
+        ws_raw = [keep.tile([P, H], U8, name="ws_raw%d" % i, align_bytes=64) for i in range(2)]
+        w3w = keep.tile([P, 2 * N], U8, name="w3w", align_bytes=64)
+        w3s = keep.tile([P, N], U8, name="w3s", align_bytes=64)
+        m_sb = [keep.tile([P, 2, S], F32, name="m_sb%d" % i) for i in range(2)]
+        l_sb = [keep.tile([P, 2, S], F32, name="l_sb%d" % i) for i in range(2)]
+        u_sb = keep.tile([P, PACK], F32, name="u_sb")
+
+        nc.vector.memset(xs[:].bitcast(I32), 0)
+        nc.gpsimd.memset(ws_raw[0][:].bitcast(I32), 0)
+        nc.gpsimd.memset(ws_raw[1][:].bitcast(I32), 0)
+        nc.gpsimd.memset(w3s[:].bitcast(I32), 0)
+
+        m_rows = minv.rearrange("(p t) j -> p t j", t=PACK)
+        l_rows = lam0.rearrange("(p t) j -> p t j", t=PACK)
+        nc.sync.dma_start(offs_sb[:], offs)
+        load_scale_rows(nc.sync, xs, x_scales[0])
+        nc.sync.dma_start(out=w_raw[0][:].bitcast(I32), in_=w1_words[0].bitcast(I32))
+        nc.sync.dma_start(out=xw[:], in_=x_words[0].rearrange("p n t -> p (n t)").bitcast(I32))
+        nc.sync.dma_start(out=w_raw[1][:].bitcast(I32), in_=w2_words[0].bitcast(I32))
+        load_scale_rows(nc.sync, ws_raw[0], w1_scales[0])
+        nc.sync.dma_start(out=m_sb[0][:], in_=m_rows[:, 0:2, :])
+        nc.sync.dma_start(out=l_sb[0][:], in_=l_rows[:, 0:2, :])
+        load_scale_rows(nc.sync, ws_raw[1], w2_scales[0])
+        nc.sync.dma_start(out=m_sb[1][:], in_=m_rows[:, 2:4, :])
+        nc.sync.dma_start(out=l_sb[1][:], in_=l_rows[:, 2:4, :])
+        nc.sync.dma_start(bod_sb[:], bod)
+        nc.sync.dma_start(out=u_sb[:], in_=unit.rearrange("(p t) o -> p (t o)", t=PACK))
+        nc.sync.dma_start(out=w3w[:].bitcast(I32), in_=w3_words[0].bitcast(I32))
+        load_scale_rows(nc.sync, w3s, w3_scales[0])
+
+        def m_of(t):
+            return m_sb[t // 2][:, t % 2, :]
+
+        def l_of(t):
+            return l_sb[t // 2][:, t % 2, :]
+
+        w_deal = [keep.tile([P, 2 * H], U8, name="w_deal%d" % i, align_bytes=64) for i in range(2)]
+        ws_deal = [keep.tile([P, H], U8, name="ws_deal%d" % i, align_bytes=64) for i in range(2)]
+
+        def deal_words(i):
+            nc.vector.tensor_copy(
+                out=w_deal[i][:].rearrange("p (t m b) -> p t m b", t=PACK, b=2),
+                in_=w_raw[i][:].rearrange("p (m t b) -> p t m b", t=PACK, b=2),
+            )
+
+        def deal_scales(i):
+            nc.vector.tensor_copy(
+                out=ws_deal[i][:].rearrange("p (t m) -> p t m", t=PACK),
+                in_=ws_raw[i][:].rearrange("p (m t) -> p t m", t=PACK),
+            )
+
+        xg = keep.tile([P, S], U32, name="xg", align_bytes=64)
+        xsg = keep.tile([P, S], U8, name="xsg", align_bytes=64)
+        deal_words(0)
+        nc.vector.tensor_copy(out=xsg[:], in_=xs[:].indirect(offs_sb[:]))
+        nc.vector.tensor_copy(out=xg[:], in_=xw[:].bitcast(U32).indirect(offs_sb[:]))
+        deal_scales(0)
+        deal_words(1)
+        deal_scales(1)
+
+        def first_product(i, t):
+            acc = psum.tile([P, S], F32, name="acc", tag="bank%d" % (4 * i + t))
+            nc.tensor.matmul_mx(
+                out=acc[:],
+                lhsT=w_deal[i][:, 2 * P * t : 2 * P * (t + 1)].bitcast(FP4X4),
+                lhsT_scale=ws_deal[i][:, P * t : P * (t + 1)],
+                rhs=xg[:].bitcast(FP8X4),
+                rhs_scale=xsg[:],
+                start=True,
+                stop=True,
+            )
+            return acc
+
+        vn = [first_product(0, t) for t in range(PACK)]
+        vt = [first_product(1, t) for t in range(PACK)]
+
+        u_mu = keep.tile([P, PACK], F32, name="u_mu")
+        u_drag = keep.tile([P, PACK], F32, name="u_drag")
+        nc.scalar.activation(out=u_mu[:], in_=u_sb[:], func=ACT.Copy, scale=MU)
+        nc.scalar.activation(out=u_drag[:], in_=u_sb[:], func=ACT.Copy, scale=-DRAG)
+
+        msq = plane_tiles("msq")
+        a = plane_tiles("a")
+        d = plane_tiles("d")
+        dg = plane_tiles("dg")
+        e = plane_tiles("e")
+        pp = plane_tiles("pp")
+        f = plane_tiles("f")
+        lam2 = plane_tiles("lam2")
+        lg = plane_tiles("lg")
+        b = plane_tiles("b")
+        g1 = plane_tiles("g1")
+        g2 = plane_tiles("g2")
+        r = keep.tile([P, PACK, S], F32, name="r")
+        drag = keep.tile([P, PACK, S], F32, name="drag")
+
+        def gather_by_bod(dst, window):
+            for h in range(2):
+                nc.scalar.activation(
+                    out=dst[:, h * HALF : (h + 1) * HALF],
+                    in_=window[:].indirect(bod_sb[:, h * HALF // 16 : (h + 1) * HALF // 16]),
+                    func=ACT.Copy,
+                )
+
+        for t in range(PACK):
+            nc.scalar.activation(out=msq[t][:], in_=m_of(t), func=ACT.Square)
+        for t in range(PACK):
+            nc.vector.tensor_tensor(out=a[t][:], in0=vn[t][:], in1=m_of(t), op=ALU.mult)
+            if t > 0:
+                nc.vector.tensor_tensor(out=d[t - 1][:], in0=l_of(t - 1), in1=a[t - 1][:], op=ALU.subtract)
+                gather_by_bod(dg[t - 1], d[t - 1])
+        t = PACK - 1
+        nc.vector.scalar_tensor_tensor(out=b[0][:], in0=vt[0][:], scalar=-1.0 / MU, in1=m_of(0), op0=ALU.mult, op1=ALU.mult)
+        nc.vector.tensor_tensor(out=d[t][:], in0=l_of(t), in1=a[t][:], op=ALU.subtract)
+        gather_by_bod(dg[t], d[t])
+        for t in range(PACK):
+            nc.vector.scalar_tensor_tensor(out=pp[t][:], in0=dg[t][:], scalar=0.0, in1=msq[t][:], op0=ALU.max, op1=ALU.mult)
+            nc.vector.scalar_tensor_tensor(out=e[t][:], in0=d[t][:], scalar=0.0, in1=a[t][:], op0=ALU.max, op1=ALU.subtract)
+            if t + 1 < PACK:
+                nc.vector.scalar_tensor_tensor(out=b[t + 1][:], in0=vt[t + 1][:], scalar=-1.0 / MU, in1=m_of(t + 1), op0=ALU.mult, op1=ALU.mult)
+            nc.vector.scalar_tensor_tensor(out=f[t][:], in0=pp[t][:], scalar=-MU, in1=e[t][:], op0=ALU.mult, op1=ALU.add)
+            nc.scalar.activation(out=lam2[t][:], in_=f[t][:], func=ACT.Relu)
+            gather_by_bod(lg[t], lam2[t])
+            nc.scalar.activation(out=drag[:, t, :], in_=vt[t][:], func=ACT.Copy, scale=u_drag[:, t : t + 1])
+        for t0 in range(0, PACK, 2):
+            for t in (t0, t0 + 1):
+                nc.vector.tensor_tensor(out=g1[t][:], in0=b[t][:], in1=lam2[t][:], op=ALU.min)
+            for t in (t0, t0 + 1):
+                nc.vector.scalar_tensor_tensor(out=g2[t][:], in0=lam2[t][:], scalar=-1.0, in1=g1[t][:], op0=ALU.mult, op1=ALU.max)
+            for t in (t0, t0 + 1):
+                nc.vector.scalar_tensor_tensor(
+                    out=r[:, t, :], in0=lg[t][:], scalar=u_mu[:, t : t + 1], in1=g2[t][:], op0=ALU.mult, op1=ALU.mult
+                )
+
+        hid, codes, scales = [], [], []
+        for c, (j0, j1) in enumerate(OUT_CHUNKS):
+            hid.append(keep.tile([P, j1 - j0, PACK], BF16, name="hid%d" % c, align_bytes=64))
+            codes.append(keep.tile([P, j1 - j0], U32, name="codes%d" % c, align_bytes=64))
+            scales.append(keep.tile([P, j1 - j0], U8, name="scales%d" % c, align_bytes=64))
+
+        def make_hid(c):
+            j0, j1 = OUT_CHUNKS[c]
+            nc.vector.tensor_tensor(
+                out=hid[c][:].rearrange("p (c i) t -> p c t i", i=4),
+                in0=r[:, :, j0:j1].rearrange("p t (c i) -> p c t i", i=4),
+                in1=drag[:, :, j0:j1].rearrange("p t (c i) -> p c t i", i=4),
+                op=ALU.add,
+            )
+
+        def finish(c):
+            j0, j1 = OUT_CHUNKS[c]
+            nc.vector.quantize_mx(out=codes[c][:].bitcast(FP8X4), scales=scales[c][:], in_=hid[c][:].rearrange("p j t -> p (j t)"))
+            acc = psum.tile([P, j1 - j0], F32, name="acc_out", tag="bank%d" % c)
+            nc.tensor.matmul_mx(
+                out=acc[:], lhsT=w3w[:].bitcast(FP4X4), lhsT_scale=w3s[:], rhs=codes[c][:].bitcast(FP8X4), rhs_scale=scales[c][:],
+                start=True, stop=True,
+            )
+            res = keep.tile([P, j1 - j0], F32, name="res%d" % c)
+            nc.scalar.copy(out=res[:], in_=acc[:])
+            nc.sync.dma_start(out=out[:, j0:j1], in_=res[:])
+
+        make_hid(0)
+        for c in range(len(OUT_CHUNKS)):
+            if c + 1 < len(OUT_CHUNKS):
+                make_hid(c + 1)
+            finish(c)

@@ -24,8 +24,8 @@ HALF = S // 2
 OUT_CHUNKS = ((0, 256), (256, 384), (384, 512))
 
 
-def load_scale_rows(queue, plane, rows):
-    for q in range(4):
+def load_scale_rows(queue, plane, rows, quadrants=range(4)):
+    for q in quadrants:
         queue.dma_start(out=plane[32 * q : 32 * q + 4, :].bitcast(I32), in_=rows[4 * q : 4 * q + 4, :].bitcast(I32))
 
 
@@ -45,33 +45,33 @@ def tile_picked_ycontc_slide_p_kernel(
         xw = keep.tile([P, T], I32, name="xw", align_bytes=64)
         xs = keep.tile([P, T], U8, name="xs", align_bytes=64)
         w_raw = [keep.tile([P, 2 * H], U8, name="w_raw%d" % i, align_bytes=64) for i in range(2)]
-        ws_raw = [keep.tile([P, H], U8, name="ws_raw%d" % i, align_bytes=64) for i in range(2)]
+        ws_all = keep.tile([P, 2 * H + N], U8, name="ws_all", align_bytes=64)
+        ws_raw = [ws_all[:, 0:H], ws_all[:, H : 2 * H]]
+        w3s = ws_all[:, 2 * H : 2 * H + N]
         w3w = keep.tile([P, 2 * N], U8, name="w3w", align_bytes=64)
-        w3s = keep.tile([P, N], U8, name="w3s", align_bytes=64)
         m_sb = [keep.tile([P, 2, S], F32, name="m_sb%d" % i) for i in range(2)]
         l_sb = [keep.tile([P, 2, S], F32, name="l_sb%d" % i) for i in range(2)]
         u_sb = keep.tile([P, PACK], F32, name="u_sb")
 
-        nc.vector.memset(xs[:].bitcast(I32), 0)
-        nc.gpsimd.memset(ws_raw[0][:].bitcast(I32), 0)
-        nc.gpsimd.memset(ws_raw[1][:].bitcast(I32), 0)
-        nc.gpsimd.memset(w3s[:].bitcast(I32), 0)
+        nc.gpsimd.memset(xs[:].bitcast(I32), 0)
+        nc.gpsimd.memset(ws_all[:].bitcast(I32), 0)
 
         m_rows = minv.rearrange("(p t) j -> p t j", t=PACK)
         l_rows = lam0.rearrange("(p t) j -> p t j", t=PACK)
         nc.sync.dma_start(offs_sb[:], offs)
-        load_scale_rows(nc.sync, xs, x_scales[0])
         nc.sync.dma_start(out=w_raw[0][:].bitcast(I32), in_=w1_words[0].bitcast(I32))
+        nc.sync.dma_start(bod_sb[:], bod)
+        nc.sync.dma_start(out=u_sb[:], in_=unit.rearrange("(p t) o -> p (t o)", t=PACK))
         nc.sync.dma_start(out=xw[:], in_=x_words[0].rearrange("p n t -> p (n t)").bitcast(I32))
-        nc.sync.dma_start(out=w_raw[1][:].bitcast(I32), in_=w2_words[0].bitcast(I32))
-        load_scale_rows(nc.sync, ws_raw[0], w1_scales[0])
+        load_scale_rows(nc.sync, xs, x_scales[0])
+        load_scale_rows(nc.sync, ws_raw[0], w1_scales[0], (0, 1))
         nc.sync.dma_start(out=m_sb[0][:], in_=m_rows[:, 0:2, :])
+        load_scale_rows(nc.sync, ws_raw[0], w1_scales[0], (2, 3))
+        nc.sync.dma_start(out=w_raw[1][:].bitcast(I32), in_=w2_words[0].bitcast(I32))
         nc.sync.dma_start(out=l_sb[0][:], in_=l_rows[:, 0:2, :])
         load_scale_rows(nc.sync, ws_raw[1], w2_scales[0])
         nc.sync.dma_start(out=m_sb[1][:], in_=m_rows[:, 2:4, :])
         nc.sync.dma_start(out=l_sb[1][:], in_=l_rows[:, 2:4, :])
-        nc.sync.dma_start(bod_sb[:], bod)
-        nc.sync.dma_start(out=u_sb[:], in_=unit.rearrange("(p t) o -> p (t o)", t=PACK))
         nc.sync.dma_start(out=w3w[:].bitcast(I32), in_=w3_words[0].bitcast(I32))
         load_scale_rows(nc.sync, w3s, w3_scales[0])
 
@@ -93,14 +93,14 @@ def tile_picked_ycontc_slide_p_kernel(
         def deal_scales(i):
             nc.vector.tensor_copy(
                 out=ws_deal[i][:].rearrange("p (t m) -> p t m", t=PACK),
-                in_=ws_raw[i][:].rearrange("p (m t) -> p t m", t=PACK),
+                in_=ws_raw[i].rearrange("p (m t) -> p t m", t=PACK),
             )
 
         xg = keep.tile([P, S], U32, name="xg", align_bytes=64)
         xsg = keep.tile([P, S], U8, name="xsg", align_bytes=64)
         deal_words(0)
-        nc.vector.tensor_copy(out=xsg[:], in_=xs[:].indirect(offs_sb[:]))
         nc.vector.tensor_copy(out=xg[:], in_=xw[:].bitcast(U32).indirect(offs_sb[:]))
+        nc.vector.tensor_copy(out=xsg[:], in_=xs[:].indirect(offs_sb[:]))
         deal_scales(0)
         deal_words(1)
         deal_scales(1)
@@ -118,8 +118,11 @@ def tile_picked_ycontc_slide_p_kernel(
             )
             return acc
 
-        vn = [first_product(0, t) for t in range(PACK)]
-        vt = [first_product(1, t) for t in range(PACK)]
+        vn, vt = [first_product(0, 0)], []
+        for t in range(PACK):
+            if t + 1 < PACK:
+                vn.append(first_product(0, t + 1))
+            vt.append(first_product(1, t))
 
         u_mu = keep.tile([P, PACK], F32, name="u_mu")
         u_drag = keep.tile([P, PACK], F32, name="u_drag")
@@ -127,11 +130,9 @@ def tile_picked_ycontc_slide_p_kernel(
         nc.scalar.activation(out=u_drag[:], in_=u_sb[:], func=ACT.Copy, scale=-DRAG)
 
         msq = plane_tiles("msq")
-        a = plane_tiles("a")
+        na = plane_tiles("na")
         d = plane_tiles("d")
         dg = plane_tiles("dg")
-        e = plane_tiles("e")
-        pp = plane_tiles("pp")
         f = plane_tiles("f")
         lam2 = plane_tiles("lam2")
         lg = plane_tiles("lg")
@@ -140,6 +141,8 @@ def tile_picked_ycontc_slide_p_kernel(
         g2 = plane_tiles("g2")
         r = keep.tile([P, PACK, S], F32, name="r")
         drag = keep.tile([P, PACK, S], F32, name="drag")
+        e = [l_of(3), l_of(2), l_of(0), l_of(1)]
+        pp = [m_of(3), m_of(2), m_of(0), m_of(1)]
 
         def gather_by_bod(dst, window):
             for h in range(2):
@@ -149,25 +152,36 @@ def tile_picked_ycontc_slide_p_kernel(
                     func=ACT.Copy,
                 )
 
+        def make_na(t):
+            nc.vector.scalar_tensor_tensor(out=na[t][:], in0=vn[t][:], scalar=-1.0, in1=m_of(t), op0=ALU.mult, op1=ALU.mult)
+
+        def make_b(t):
+            nc.vector.scalar_tensor_tensor(out=b[t][:], in0=vt[t][:], scalar=-1.0 / MU, in1=m_of(t), op0=ALU.mult, op1=ALU.mult)
+
+        def make_d(t, engine):
+            engine.tensor_tensor(out=d[t][:], in0=l_of(t), in1=na[t][:], op=ALU.add)
+
         for t in range(PACK):
             nc.scalar.activation(out=msq[t][:], in_=m_of(t), func=ACT.Square)
+        last = PACK - 1
+        make_na(0)
+        for t in range(last):
+            make_d(t, nc.gpsimd)
+            make_na(t + 1)
+            make_b(t)
+        make_b(last)
+        make_d(last, nc.vector)
         for t in range(PACK):
-            nc.vector.tensor_tensor(out=a[t][:], in0=vn[t][:], in1=m_of(t), op=ALU.mult)
-            if t > 0:
-                nc.vector.tensor_tensor(out=d[t - 1][:], in0=l_of(t - 1), in1=a[t - 1][:], op=ALU.subtract)
-                gather_by_bod(dg[t - 1], d[t - 1])
-        t = PACK - 1
-        nc.vector.scalar_tensor_tensor(out=b[0][:], in0=vt[0][:], scalar=-1.0 / MU, in1=m_of(0), op0=ALU.mult, op1=ALU.mult)
-        nc.vector.tensor_tensor(out=d[t][:], in0=l_of(t), in1=a[t][:], op=ALU.subtract)
-        gather_by_bod(dg[t], d[t])
+            gather_by_bod(dg[t], d[t])
+        for t0 in range(0, PACK, 2):
+            for t in (t0, t0 + 1):
+                nc.vector.scalar_tensor_tensor(out=pp[t], in0=dg[t][:], scalar=0.0, in1=msq[t][:], op0=ALU.max, op1=ALU.mult)
+                nc.vector.scalar_tensor_tensor(out=e[t], in0=d[t][:], scalar=0.0, in1=na[t][:], op0=ALU.max, op1=ALU.add)
+            for t in (t0, t0 + 1):
+                nc.vector.scalar_tensor_tensor(out=f[t][:], in0=pp[t], scalar=-MU, in1=e[t], op0=ALU.mult, op1=ALU.add)
+                nc.scalar.activation(out=lam2[t][:], in_=f[t][:], func=ACT.Relu)
+                gather_by_bod(lg[t], lam2[t])
         for t in range(PACK):
-            nc.vector.scalar_tensor_tensor(out=pp[t][:], in0=dg[t][:], scalar=0.0, in1=msq[t][:], op0=ALU.max, op1=ALU.mult)
-            nc.vector.scalar_tensor_tensor(out=e[t][:], in0=d[t][:], scalar=0.0, in1=a[t][:], op0=ALU.max, op1=ALU.subtract)
-            if t + 1 < PACK:
-                nc.vector.scalar_tensor_tensor(out=b[t + 1][:], in0=vt[t + 1][:], scalar=-1.0 / MU, in1=m_of(t + 1), op0=ALU.mult, op1=ALU.mult)
-            nc.vector.scalar_tensor_tensor(out=f[t][:], in0=pp[t][:], scalar=-MU, in1=e[t][:], op0=ALU.mult, op1=ALU.add)
-            nc.scalar.activation(out=lam2[t][:], in_=f[t][:], func=ACT.Relu)
-            gather_by_bod(lg[t], lam2[t])
             nc.scalar.activation(out=drag[:, t, :], in_=vt[t][:], func=ACT.Copy, scale=u_drag[:, t : t + 1])
         for t0 in range(0, PACK, 2):
             for t in (t0, t0 + 1):
@@ -199,7 +213,7 @@ def tile_picked_ycontc_slide_p_kernel(
             nc.vector.quantize_mx(out=codes[c][:].bitcast(FP8X4), scales=scales[c][:], in_=hid[c][:].rearrange("p j t -> p (j t)"))
             acc = psum.tile([P, j1 - j0], F32, name="acc_out", tag="bank%d" % c)
             nc.tensor.matmul_mx(
-                out=acc[:], lhsT=w3w[:].bitcast(FP4X4), lhsT_scale=w3s[:], rhs=codes[c][:].bitcast(FP8X4), rhs_scale=scales[c][:],
+                out=acc[:], lhsT=w3w[:].bitcast(FP4X4), lhsT_scale=w3s, rhs=codes[c][:].bitcast(FP8X4), rhs_scale=scales[c][:],
                 start=True, stop=True,
             )
             res = keep.tile([P, j1 - j0], F32, name="res%d" % c)
@@ -207,7 +221,8 @@ def tile_picked_ycontc_slide_p_kernel(
             nc.sync.dma_start(out=out[:, j0:j1], in_=res[:])
 
         make_hid(0)
-        for c in range(len(OUT_CHUNKS)):
-            if c + 1 < len(OUT_CHUNKS):
-                make_hid(c + 1)
-            finish(c)
+        make_hid(1)
+        finish(0)
+        make_hid(2)
+        finish(1)
+        finish(2)

@@ -1,6 +1,7 @@
 from contextlib import ExitStack
 
 import concourse.mybir as mybir
+from concourse.masks import make_identity
 
 K, T, S, N, H = 512, 1024, 512, 128, 512
 FLOPS = 2 * K * H * S * 2 + 2 * H * N * S
@@ -55,6 +56,8 @@ def tile_picked_ycontc_slide_p_kernel(
 
         nc.gpsimd.memset(xs[:].bitcast(I32), 0)
         nc.gpsimd.memset(ws_all[:].bitcast(I32), 0)
+        ident = keep.tile([P, P], F32, name="ident")
+        make_identity(nc, ident[:])
 
         m_rows = minv.rearrange("(p t) j -> p t j", t=PACK)
         l_rows = lam0.rearrange("(p t) j -> p t j", t=PACK)
@@ -133,7 +136,6 @@ def tile_picked_ycontc_slide_p_kernel(
         na = plane_tiles("na")
         d = plane_tiles("d")
         dg = plane_tiles("dg")
-        f = plane_tiles("f")
         lam2 = plane_tiles("lam2")
         lg = plane_tiles("lg")
         b = plane_tiles("b")
@@ -144,12 +146,13 @@ def tile_picked_ycontc_slide_p_kernel(
         e = [l_of(3), l_of(2), l_of(0), l_of(1)]
         pp = [m_of(3), m_of(2), m_of(0), m_of(1)]
 
-        def gather_by_bod(dst, window):
+        def gather_by_bod(dst, window, scale):
             for h in range(2):
                 nc.scalar.activation(
                     out=dst[:, h * HALF : (h + 1) * HALF],
                     in_=window[:].indirect(bod_sb[:, h * HALF // 16 : (h + 1) * HALF // 16]),
                     func=ACT.Copy,
+                    scale=scale,
                 )
 
         def make_na(t):
@@ -172,26 +175,62 @@ def tile_picked_ycontc_slide_p_kernel(
         make_b(last)
         make_d(last, nc.vector)
         for t in range(PACK):
-            gather_by_bod(dg[t], d[t])
-        for t0 in range(0, PACK, 2):
-            for t in (t0, t0 + 1):
-                nc.vector.scalar_tensor_tensor(out=pp[t], in0=dg[t][:], scalar=0.0, in1=msq[t][:], op0=ALU.max, op1=ALU.mult)
-                nc.vector.scalar_tensor_tensor(out=e[t], in0=d[t][:], scalar=0.0, in1=na[t][:], op0=ALU.max, op1=ALU.add)
-            for t in (t0, t0 + 1):
-                nc.vector.scalar_tensor_tensor(out=f[t][:], in0=pp[t], scalar=-MU, in1=e[t], op0=ALU.mult, op1=ALU.add)
-                nc.scalar.activation(out=lam2[t][:], in_=f[t][:], func=ACT.Relu)
-                gather_by_bod(lg[t], lam2[t])
+            gather_by_bod(dg[t], d[t], -MU)
+
+        def turn(dst, src, start, stop):
+            for c in range(PACK):
+                cols = slice(P * c, P * (c + 1))
+                nc.tensor.matmul(
+                    out=dst[:, cols], lhsT=src[:, cols], rhs=ident[:], is_transpose=True,
+                    start=start and c == 0, stop=stop and c == PACK - 1,
+                )
+
+        cone = []
+        for t in range(PACK):
+            nc.vector.scalar_tensor_tensor(out=pp[t], in0=dg[t][:], scalar=0.0, in1=msq[t][:], op0=ALU.min, op1=ALU.mult)
+            nc.vector.scalar_tensor_tensor(out=e[t], in0=d[t][:], scalar=0.0, in1=na[t][:], op0=ALU.max, op1=ALU.add)
+            if t < 2:
+                f_turned = psum.tile([P, S], F32, name="f_turned", tag="bank%d" % t)
+                turn(f_turned, pp[t], True, False)
+                turn(f_turned, e[t], False, True)
+                lam2_turned = drag[:, 2 + t, :]
+                nc.scalar.activation(out=lam2_turned, in_=f_turned[:], func=ACT.Relu)
+                back = psum.tile([P, S], F32, name="back", tag="bank%d" % t)
+                turn(back, lam2_turned, True, True)
+                nc.scalar.copy(out=lam2[t][:], in_=back[:])
+                cone.append(back)
+        for t, f in ((2, na[3]), (3, na[0])):
+            nc.gpsimd.tensor_tensor(out=f[:], in0=e[t], in1=pp[t], op=ALU.add)
+            nc.scalar.activation(out=lam2[t][:], in_=f[:], func=ACT.Relu)
+            cone.append(lam2[t])
+        for t in range(PACK):
+            gather_by_bod(lg[t], lam2[t], 1.0)
         for t in range(PACK):
             nc.scalar.activation(out=drag[:, t, :], in_=vt[t][:], func=ACT.Copy, scale=u_drag[:, t : t + 1])
-        for t0 in range(0, PACK, 2):
-            for t in (t0, t0 + 1):
-                nc.vector.tensor_tensor(out=g1[t][:], in0=b[t][:], in1=lam2[t][:], op=ALU.min)
-            for t in (t0, t0 + 1):
-                nc.vector.scalar_tensor_tensor(out=g2[t][:], in0=lam2[t][:], scalar=-1.0, in1=g1[t][:], op0=ALU.mult, op1=ALU.max)
-            for t in (t0, t0 + 1):
-                nc.vector.scalar_tensor_tensor(
-                    out=r[:, t, :], in0=lg[t][:], scalar=u_mu[:, t : t + 1], in1=g2[t][:], op0=ALU.mult, op1=ALU.mult
-                )
+
+        def clip_above(t):
+            nc.vector.tensor_tensor(out=g1[t][:], in0=cone[t][:], in1=b[t][:], op=ALU.min)
+
+        def clip_below(t):
+            nc.vector.scalar_tensor_tensor(out=g2[t][:], in0=cone[t][:], scalar=-1.0, in1=g1[t][:], op0=ALU.mult, op1=ALU.max)
+
+        def make_r(t):
+            nc.vector.scalar_tensor_tensor(
+                out=r[:, t, :], in0=lg[t][:], scalar=u_mu[:, t : t + 1], in1=g2[t][:], op0=ALU.mult, op1=ALU.mult
+            )
+
+        clip_above(0)
+        clip_above(1)
+        clip_below(0)
+        clip_below(1)
+        make_r(0)
+        clip_above(2)
+        make_r(1)
+        clip_above(3)
+        clip_below(2)
+        clip_below(3)
+        make_r(2)
+        make_r(3)
 
         hid, codes, scales = [], [], []
         for c, (j0, j1) in enumerate(OUT_CHUNKS):
@@ -202,16 +241,16 @@ def tile_picked_ycontc_slide_p_kernel(
         def make_hid(c):
             j0, j1 = OUT_CHUNKS[c]
             nc.vector.tensor_tensor(
-                out=hid[c][:].rearrange("p (c i) t -> p c t i", i=4),
-                in0=r[:, :, j0:j1].rearrange("p t (c i) -> p c t i", i=4),
-                in1=drag[:, :, j0:j1].rearrange("p t (c i) -> p c t i", i=4),
+                out=hid[c][:].rearrange("p (c i) t -> p c t i", i=2),
+                in0=r[:, :, j0:j1].rearrange("p t (c i) -> p c t i", i=2),
+                in1=drag[:, :, j0:j1].rearrange("p t (c i) -> p c t i", i=2),
                 op=ALU.add,
             )
 
         def finish(c):
             j0, j1 = OUT_CHUNKS[c]
             nc.vector.quantize_mx(out=codes[c][:].bitcast(FP8X4), scales=scales[c][:], in_=hid[c][:].rearrange("p j t -> p (j t)"))
-            acc = psum.tile([P, j1 - j0], F32, name="acc_out", tag="bank%d" % c)
+            acc = psum.tile([P, j1 - j0], F32, name="acc_out", tag="bank%d" % ((c + 2) % PACK))
             nc.tensor.matmul_mx(
                 out=acc[:], lhsT=w3w[:].bitcast(FP4X4), lhsT_scale=w3s, rhs=codes[c][:].bitcast(FP8X4), rhs_scale=scales[c][:],
                 start=True, stop=True,

@@ -22,6 +22,7 @@ PACK = 4
 MU = 0.6
 DRAG = 0.4
 HALF = S // 2
+SPARE = 16
 OUT_CHUNKS = ((0, 256), (256, 384), (384, 512))
 
 
@@ -132,12 +133,14 @@ def tile_picked_ycontc_slide_p_kernel(
         nc.scalar.activation(out=u_mu[:], in_=u_sb[:], func=ACT.Copy, scale=MU)
         nc.scalar.activation(out=u_drag[:], in_=u_sb[:], func=ACT.Copy, scale=-DRAG)
 
-        msq = plane_tiles("msq")
         na = plane_tiles("na")
-        d = plane_tiles("d")
+        d_wide = [keep.tile([P, S + SPARE], F32, name="d_wide%d" % t) for t in range(PACK)]
+        d = [w[:, 0:S] for w in d_wide]
         dg = plane_tiles("dg")
-        lam2 = plane_tiles("lam2")
-        lg = plane_tiles("lg")
+        lam2_wide = [keep.tile([P, S + SPARE], F32, name="lam2_wide%d" % t) for t in range(PACK)]
+        lam2 = [w[:, 0:S] for w in lam2_wide]
+        for w in d_wide + lam2_wide:
+            nc.gpsimd.memset(w[:, S : S + SPARE], 0.0)
         b = plane_tiles("b")
         g1 = plane_tiles("g1")
         g2 = plane_tiles("g2")
@@ -145,15 +148,23 @@ def tile_picked_ycontc_slide_p_kernel(
         drag = keep.tile([P, PACK, S], F32, name="drag")
         e = [l_of(3), l_of(2), l_of(0), l_of(1)]
         pp = [m_of(3), m_of(2), m_of(0), m_of(1)]
+        msq_own = keep.tile([P, 2, S], F32, name="msq_own")
+        msq = [msq_own[:, 0, :], msq_own[:, 1, :], drag[:, 2, :], drag[:, 3, :]]
+        lam2_turned = [keep.tile([P, S], F32, name="lam2_turned%d" % t) for t in range(2)]
+        lg_own = keep.tile([P, 3, S], F32, name="lg_own")
+        lg = [lg_own[:, 0, :], na[3][:], lg_own[:, 1, :], lg_own[:, 2, :]]
 
-        def gather_by_bod(dst, window, scale):
-            for h in range(2):
+        def gather_by_bod(dst, window, scale, halves=range(2)):
+            for h in halves:
                 nc.scalar.activation(
                     out=dst[:, h * HALF : (h + 1) * HALF],
                     in_=window[:].indirect(bod_sb[:, h * HALF // 16 : (h + 1) * HALF // 16]),
                     func=ACT.Copy,
                     scale=scale,
                 )
+
+        def gather_whole(dst, window, scale):
+            nc.scalar.activation(out=dst[:], in_=window[:].indirect(bod_sb[:]), func=ACT.Copy, scale=scale)
 
         def make_na(t):
             nc.vector.scalar_tensor_tensor(out=na[t][:], in0=vn[t][:], scalar=-1.0, in1=m_of(t), op0=ALU.mult, op1=ALU.mult)
@@ -165,7 +176,7 @@ def tile_picked_ycontc_slide_p_kernel(
             engine.tensor_tensor(out=d[t][:], in0=l_of(t), in1=na[t][:], op=ALU.add)
 
         for t in range(PACK):
-            nc.scalar.activation(out=msq[t][:], in_=m_of(t), func=ACT.Square)
+            nc.scalar.activation(out=msq[t], in_=m_of(t), func=ACT.Square)
         last = PACK - 1
         make_na(0)
         for t in range(last):
@@ -175,7 +186,7 @@ def tile_picked_ycontc_slide_p_kernel(
         make_b(last)
         make_d(last, nc.vector)
         for t in range(PACK):
-            gather_by_bod(dg[t], d[t], -MU)
+            gather_whole(dg[t], d_wide[t], -MU)
 
         def turn(dst, src, start, stop):
             for c in range(PACK):
@@ -187,25 +198,27 @@ def tile_picked_ycontc_slide_p_kernel(
 
         cone = []
         for t in range(PACK):
-            nc.vector.scalar_tensor_tensor(out=pp[t], in0=dg[t][:], scalar=0.0, in1=msq[t][:], op0=ALU.min, op1=ALU.mult)
+            nc.vector.scalar_tensor_tensor(out=pp[t], in0=dg[t][:], scalar=0.0, in1=msq[t], op0=ALU.min, op1=ALU.mult)
             nc.vector.scalar_tensor_tensor(out=e[t], in0=d[t][:], scalar=0.0, in1=na[t][:], op0=ALU.max, op1=ALU.add)
             if t < 2:
                 f_turned = psum.tile([P, S], F32, name="f_turned", tag="bank%d" % t)
                 turn(f_turned, pp[t], True, False)
                 turn(f_turned, e[t], False, True)
-                lam2_turned = drag[:, 2 + t, :]
-                nc.scalar.activation(out=lam2_turned, in_=f_turned[:], func=ACT.Relu)
+                nc.scalar.activation(out=lam2_turned[t][:], in_=f_turned[:], func=ACT.Relu)
                 back = psum.tile([P, S], F32, name="back", tag="bank%d" % t)
-                turn(back, lam2_turned, True, True)
+                turn(back, lam2_turned[t], True, True)
                 nc.scalar.copy(out=lam2[t][:], in_=back[:])
                 cone.append(back)
-        for t, f in ((2, na[3]), (3, na[0])):
-            nc.gpsimd.tensor_tensor(out=f[:], in0=e[t], in1=pp[t], op=ALU.add)
-            nc.scalar.activation(out=lam2[t][:], in_=f[:], func=ACT.Relu)
+        for t, f in ((2, na[3][:]), (3, na[0][:])):
+            nc.gpsimd.tensor_tensor(out=f, in0=e[t], in1=pp[t], op=ALU.add)
+            nc.scalar.activation(out=lam2[t][:], in_=f, func=ACT.Relu)
             cone.append(lam2[t])
-        for t in range(PACK):
-            gather_by_bod(lg[t], lam2[t], 1.0)
-        for t in range(PACK):
+        for t in range(2):
+            gather_whole(lg[t], lam2_wide[t], 1.0)
+        for h in range(2):
+            for t in (2, 3):
+                gather_by_bod(lg[t], lam2_wide[t], 1.0, (h,))
+        for t in range(3):
             nc.scalar.activation(out=drag[:, t, :], in_=vt[t][:], func=ACT.Copy, scale=u_drag[:, t : t + 1])
 
         def clip_above(t):
@@ -214,23 +227,24 @@ def tile_picked_ycontc_slide_p_kernel(
         def clip_below(t):
             nc.vector.scalar_tensor_tensor(out=g2[t][:], in0=cone[t][:], scalar=-1.0, in1=g1[t][:], op0=ALU.mult, op1=ALU.max)
 
-        def make_r(t):
+        def make_r(t, cols=slice(0, S)):
             nc.vector.scalar_tensor_tensor(
-                out=r[:, t, :], in0=lg[t][:], scalar=u_mu[:, t : t + 1], in1=g2[t][:], op0=ALU.mult, op1=ALU.mult
+                out=r[:, t, cols], in0=lg[t][:, cols], scalar=u_mu[:, t : t + 1], in1=g2[t][:, cols], op0=ALU.mult, op1=ALU.mult
             )
 
+        nc.vector.tensor_scalar(out=drag[:, 3, :], in0=vt[3][:], scalar1=u_drag[:, 3:4], scalar2=None, op0=ALU.mult)
         clip_above(0)
-        clip_above(1)
         clip_below(0)
+        clip_above(1)
         clip_below(1)
-        make_r(0)
         clip_above(2)
-        make_r(1)
-        clip_above(3)
+        make_r(0)
         clip_below(2)
+        clip_above(3)
+        make_r(2, slice(0, HALF))
         clip_below(3)
-        make_r(2)
-        make_r(3)
+        make_r(1)
+        make_r(3, slice(0, HALF))
 
         hid, codes, scales = [], [], []
         for c, (j0, j1) in enumerate(OUT_CHUNKS):
@@ -260,8 +274,10 @@ def tile_picked_ycontc_slide_p_kernel(
             nc.sync.dma_start(out=out[:, j0:j1], in_=res[:])
 
         make_hid(0)
-        make_hid(1)
+        make_r(2, slice(HALF, S))
+        make_r(3, slice(HALF, S))
         finish(0)
+        make_hid(1)
         make_hid(2)
         finish(1)
         finish(2)

from contextlib import ExitStack

import concourse.mybir as mybir
from concourse.masks import make_identity

K, T, S, N, H = 512, 1024, 512, 128, 512
FLOPS = 2 * K * H * S * 2 + 2 * H * N * S

F32 = mybir.dt.float32
BF16 = mybir.dt.bfloat16
I32 = mybir.dt.int32
U32 = mybir.dt.uint32
U16 = mybir.dt.uint16
U8 = mybir.dt.uint8
FP8X4 = mybir.dt.float8_e4m3fn_x4
FP4X4 = mybir.dt.float4_e2m1fn_x4
ALU = mybir.AluOpType
ACT = mybir.ActivationFunctionType

P = 128
PACK = 4
MU = 0.6
DRAG = 0.4
HALF = S // 2
SPARE = 16
OUT_CHUNKS = ((0, 256), (256, 384), (384, 512))


def load_scale_rows(queue, plane, rows, quadrants=range(4)):
    for q in quadrants:
        queue.dma_start(out=plane[32 * q : 32 * q + 4, :].bitcast(I32), in_=rows[4 * q : 4 * q + 4, :].bitcast(I32))


def tile_picked_ycontc_slide_p_kernel(
    tc, x_words, x_scales, w1_words, w1_scales, w2_words, w2_scales, minv, lam0, unit, w3_words, w3_scales, offs, bod, out
):
    nc = tc.nc
    with ExitStack() as ctx:
        keep = ctx.enter_context(tc.tile_pool(name="keep", bufs=1))
        psum = ctx.enter_context(tc.psum_pool(name="psum", bufs=1))

        def plane_tiles(name, dtype=F32):
            return [keep.tile([P, S], dtype, name="%s%d" % (name, t), align_bytes=64) for t in range(PACK)]

        offs_sb = keep.tile([P, S // 16], U16, name="offs_sb")
        bod_sb = keep.tile([P, S // 16], U16, name="bod_sb")
        xw = keep.tile([P, T], I32, name="xw", align_bytes=64)
        xs = keep.tile([P, T], U8, name="xs", align_bytes=64)
        w_raw = [keep.tile([P, 2 * H], U8, name="w_raw%d" % i, align_bytes=64) for i in range(2)]
        ws_all = keep.tile([P, 2 * H + N], U8, name="ws_all", align_bytes=64)
        ws_raw = [ws_all[:, 0:H], ws_all[:, H : 2 * H]]
        w3s = ws_all[:, 2 * H : 2 * H + N]
        w3w = keep.tile([P, 2 * N], U8, name="w3w", align_bytes=64)
        m_sb = [keep.tile([P, 2, S], F32, name="m_sb%d" % i) for i in range(2)]
        l_sb = [keep.tile([P, 2, S], F32, name="l_sb%d" % i) for i in range(2)]
        u_sb = keep.tile([P, PACK], F32, name="u_sb")

        nc.gpsimd.memset(xs[:].bitcast(I32), 0)
        nc.gpsimd.memset(ws_all[:].bitcast(I32), 0)
        ident = keep.tile([P, P], F32, name="ident")
        make_identity(nc, ident[:])

        m_rows = minv.rearrange("(p t) j -> p t j", t=PACK)
        l_rows = lam0.rearrange("(p t) j -> p t j", t=PACK)
        nc.sync.dma_start(offs_sb[:], offs)
        nc.sync.dma_start(out=w_raw[0][:].bitcast(I32), in_=w1_words[0].bitcast(I32))
        nc.sync.dma_start(bod_sb[:], bod)
        nc.sync.dma_start(out=u_sb[:], in_=unit.rearrange("(p t) o -> p (t o)", t=PACK))
        nc.sync.dma_start(out=xw[:], in_=x_words[0].rearrange("p n t -> p (n t)").bitcast(I32))
        load_scale_rows(nc.sync, xs, x_scales[0])
        load_scale_rows(nc.sync, ws_raw[0], w1_scales[0], (0, 1))
        nc.sync.dma_start(out=m_sb[0][:], in_=m_rows[:, 0:2, :])
        load_scale_rows(nc.sync, ws_raw[0], w1_scales[0], (2, 3))
        nc.sync.dma_start(out=w_raw[1][:].bitcast(I32), in_=w2_words[0].bitcast(I32))
        nc.sync.dma_start(out=l_sb[0][:], in_=l_rows[:, 0:2, :])
        load_scale_rows(nc.sync, ws_raw[1], w2_scales[0])
        nc.sync.dma_start(out=m_sb[1][:], in_=m_rows[:, 2:4, :])
        nc.sync.dma_start(out=l_sb[1][:], in_=l_rows[:, 2:4, :])
        nc.sync.dma_start(out=w3w[:].bitcast(I32), in_=w3_words[0].bitcast(I32))
        load_scale_rows(nc.sync, w3s, w3_scales[0])

        def m_of(t):
            return m_sb[t // 2][:, t % 2, :]

        def l_of(t):
            return l_sb[t // 2][:, t % 2, :]

        w_deal = [keep.tile([P, 2 * H], U8, name="w_deal%d" % i, align_bytes=64) for i in range(2)]
        ws_deal = [keep.tile([P, H], U8, name="ws_deal%d" % i, align_bytes=64) for i in range(2)]

        def deal_words(i):
            nc.vector.tensor_copy(
                out=w_deal[i][:].rearrange("p (t m b) -> p t m b", t=PACK, b=2),
                in_=w_raw[i][:].rearrange("p (m t b) -> p t m b", t=PACK, b=2),
            )

        def deal_scales(i):
            nc.vector.tensor_copy(
                out=ws_deal[i][:].rearrange("p (t m) -> p t m", t=PACK),
                in_=ws_raw[i].rearrange("p (m t) -> p t m", t=PACK),
            )

        xg = keep.tile([P, S], U32, name="xg", align_bytes=64)
        xsg = keep.tile([P, S], U8, name="xsg", align_bytes=64)
        deal_words(0)
        nc.vector.tensor_copy(out=xg[:], in_=xw[:].bitcast(U32).indirect(offs_sb[:]))
        nc.vector.tensor_copy(out=xsg[:], in_=xs[:].indirect(offs_sb[:]))
        deal_scales(0)
        deal_words(1)
        deal_scales(1)

        def first_product(i, t):
            acc = psum.tile([P, S], F32, name="acc", tag="bank%d" % (4 * i + t))
            nc.tensor.matmul_mx(
                out=acc[:],
                lhsT=w_deal[i][:, 2 * P * t : 2 * P * (t + 1)].bitcast(FP4X4),
                lhsT_scale=ws_deal[i][:, P * t : P * (t + 1)],
                rhs=xg[:].bitcast(FP8X4),
                rhs_scale=xsg[:],
                start=True,
                stop=True,
            )
            return acc

        vn, vt = [first_product(0, 0)], []
        for t in range(PACK):
            if t + 1 < PACK:
                vn.append(first_product(0, t + 1))
            vt.append(first_product(1, t))

        u_mu = keep.tile([P, PACK], F32, name="u_mu")
        u_drag = keep.tile([P, PACK], F32, name="u_drag")
        nc.scalar.activation(out=u_mu[:], in_=u_sb[:], func=ACT.Copy, scale=MU)
        nc.scalar.activation(out=u_drag[:], in_=u_sb[:], func=ACT.Copy, scale=-DRAG)

        na = plane_tiles("na")
        d_wide = [keep.tile([P, S + SPARE], F32, name="d_wide%d" % t) for t in range(PACK)]
        d = [w[:, 0:S] for w in d_wide]
        dg = plane_tiles("dg")
        lam2_wide = [keep.tile([P, S + SPARE], F32, name="lam2_wide%d" % t) for t in range(PACK)]
        lam2 = [w[:, 0:S] for w in lam2_wide]
        for w in d_wide + lam2_wide:
            nc.gpsimd.memset(w[:, S : S + SPARE], 0.0)
        b = plane_tiles("b")
        g1 = plane_tiles("g1")
        g2 = plane_tiles("g2")
        r = keep.tile([P, PACK, S], F32, name="r")
        drag = keep.tile([P, PACK, S], F32, name="drag")
        e = [l_of(3), l_of(2), l_of(0), l_of(1)]
        pp = [m_of(3), m_of(2), m_of(0), m_of(1)]
        msq_own = keep.tile([P, 2, S], F32, name="msq_own")
        msq = [msq_own[:, 0, :], msq_own[:, 1, :], drag[:, 2, :], drag[:, 3, :]]
        lam2_turned = [keep.tile([P, S], F32, name="lam2_turned%d" % t) for t in range(2)]
        lg_own = keep.tile([P, 3, S], F32, name="lg_own")
        lg = [lg_own[:, 0, :], na[3][:], lg_own[:, 1, :], lg_own[:, 2, :]]

        def gather_by_bod(dst, window, scale, halves=range(2)):
            for h in halves:
                nc.scalar.activation(
                    out=dst[:, h * HALF : (h + 1) * HALF],
                    in_=window[:].indirect(bod_sb[:, h * HALF // 16 : (h + 1) * HALF // 16]),
                    func=ACT.Copy,
                    scale=scale,
                )

        def gather_whole(dst, window, scale):
            nc.scalar.activation(out=dst[:], in_=window[:].indirect(bod_sb[:]), func=ACT.Copy, scale=scale)

        def make_na(t):
            nc.vector.scalar_tensor_tensor(out=na[t][:], in0=vn[t][:], scalar=-1.0, in1=m_of(t), op0=ALU.mult, op1=ALU.mult)

        def make_b(t):
            nc.vector.scalar_tensor_tensor(out=b[t][:], in0=vt[t][:], scalar=-1.0 / MU, in1=m_of(t), op0=ALU.mult, op1=ALU.mult)

        def make_d(t, engine):
            engine.tensor_tensor(out=d[t][:], in0=l_of(t), in1=na[t][:], op=ALU.add)

        for t in range(PACK):
            nc.scalar.activation(out=msq[t], in_=m_of(t), func=ACT.Square)
        last = PACK - 1
        make_na(0)
        for t in range(last):
            make_d(t, nc.gpsimd)
            make_na(t + 1)
            make_b(t)
        make_b(last)
        make_d(last, nc.vector)
        for t in range(PACK):
            gather_whole(dg[t], d_wide[t], -MU)

        def turn(dst, src, start, stop):
            for c in range(PACK):
                cols = slice(P * c, P * (c + 1))
                nc.tensor.matmul(
                    out=dst[:, cols], lhsT=src[:, cols], rhs=ident[:], is_transpose=True,
                    start=start and c == 0, stop=stop and c == PACK - 1,
                )

        cone = []
        for t in range(PACK):
            nc.vector.scalar_tensor_tensor(out=pp[t], in0=dg[t][:], scalar=0.0, in1=msq[t], op0=ALU.min, op1=ALU.mult)
            nc.vector.scalar_tensor_tensor(out=e[t], in0=d[t][:], scalar=0.0, in1=na[t][:], op0=ALU.max, op1=ALU.add)
            if t < 2:
                f_turned = psum.tile([P, S], F32, name="f_turned", tag="bank%d" % t)
                turn(f_turned, pp[t], True, False)
                turn(f_turned, e[t], False, True)
                nc.scalar.activation(out=lam2_turned[t][:], in_=f_turned[:], func=ACT.Relu)
                back = psum.tile([P, S], F32, name="back", tag="bank%d" % t)
                turn(back, lam2_turned[t], True, True)
                nc.scalar.copy(out=lam2[t][:], in_=back[:])
                cone.append(back)
        for t, f in ((2, na[3][:]), (3, na[0][:])):
            nc.gpsimd.tensor_tensor(out=f, in0=e[t], in1=pp[t], op=ALU.add)
            nc.scalar.activation(out=lam2[t][:], in_=f, func=ACT.Relu)
            cone.append(lam2[t])
        for t in range(2):
            gather_whole(lg[t], lam2_wide[t], 1.0)
        for h in range(2):
            for t in (2, 3):
                gather_by_bod(lg[t], lam2_wide[t], 1.0, (h,))
        for t in range(3):
            nc.scalar.activation(out=drag[:, t, :], in_=vt[t][:], func=ACT.Copy, scale=u_drag[:, t : t + 1])

        def clip_above(t):
            nc.vector.tensor_tensor(out=g1[t][:], in0=cone[t][:], in1=b[t][:], op=ALU.min)

        def clip_below(t):
            nc.vector.scalar_tensor_tensor(out=g2[t][:], in0=cone[t][:], scalar=-1.0, in1=g1[t][:], op0=ALU.mult, op1=ALU.max)

        def make_r(t, cols=slice(0, S)):
            nc.vector.scalar_tensor_tensor(
                out=r[:, t, cols], in0=lg[t][:, cols], scalar=u_mu[:, t : t + 1], in1=g2[t][:, cols], op0=ALU.mult, op1=ALU.mult
            )

        nc.vector.tensor_scalar(out=drag[:, 3, :], in0=vt[3][:], scalar1=u_drag[:, 3:4], scalar2=None, op0=ALU.mult)
        clip_above(0)
        clip_below(0)
        clip_above(1)
        clip_below(1)
        clip_above(2)
        make_r(0)
        clip_below(2)
        clip_above(3)
        make_r(2, slice(0, HALF))
        clip_below(3)
        make_r(1)
        make_r(3, slice(0, HALF))

        hid, codes, scales = [], [], []
        for c, (j0, j1) in enumerate(OUT_CHUNKS):
            hid.append(keep.tile([P, j1 - j0, PACK], BF16, name="hid%d" % c, align_bytes=64))
            codes.append(keep.tile([P, j1 - j0], U32, name="codes%d" % c, align_bytes=64))
            scales.append(keep.tile([P, j1 - j0], U8, name="scales%d" % c, align_bytes=64))

        def make_hid(c):
            j0, j1 = OUT_CHUNKS[c]
            nc.vector.tensor_tensor(
                out=hid[c][:].rearrange("p (c i) t -> p c t i", i=2),
                in0=r[:, :, j0:j1].rearrange("p t (c i) -> p c t i", i=2),
                in1=drag[:, :, j0:j1].rearrange("p t (c i) -> p c t i", i=2),
                op=ALU.add,
            )

        def finish(c):
            j0, j1 = OUT_CHUNKS[c]
            nc.vector.quantize_mx(out=codes[c][:].bitcast(FP8X4), scales=scales[c][:], in_=hid[c][:].rearrange("p j t -> p (j t)"))
            acc = psum.tile([P, j1 - j0], F32, name="acc_out", tag="bank%d" % ((c + 2) % PACK))
            nc.tensor.matmul_mx(
                out=acc[:], lhsT=w3w[:].bitcast(FP4X4), lhsT_scale=w3s, rhs=codes[c][:].bitcast(FP8X4), rhs_scale=scales[c][:],
                start=True, stop=True,
            )
            res = keep.tile([P, j1 - j0], F32, name="res%d" % c)
            nc.scalar.copy(out=res[:], in_=acc[:])
            nc.sync.dma_start(out=out[:, j0:j1], in_=res[:])

        make_hid(0)
        make_r(2, slice(HALF, S))
        make_r(3, slice(HALF, S))
        finish(0)
        make_hid(1)
        make_hid(2)
        finish(1)
        finish(2)
